import numpy as np
import ml_dtypes


def mxq(x, axis, fmt="e4m3"):
    dtype, down = {"e4m3": (ml_dtypes.float8_e4m3fn, 7), "e5m2": (ml_dtypes.float8_e5m2, 14)}[fmt]
    v = np.moveaxis(np.asarray(x, np.float32).astype(ml_dtypes.bfloat16).astype(np.float64), axis, -1)
    blocks = v.reshape(v.shape[:-1] + (-1, 32))
    amax = np.abs(blocks).max(-1, keepdims=True)
    byte = np.maximum(np.where(amax > 0, np.frexp(amax)[1] - 1 + 127, 0) - down, 1)
    scale = np.exp2(byte - 127.0)
    codes = (blocks / scale).astype(np.float32).astype(dtype).astype(np.float64)
    return np.moveaxis((codes * scale).reshape(v.shape), -1, axis)


WIDE = False


def mx_kscale(k):
    if not WIDE:
        return np.ones(k)
    levels = np.array([30, -30])
    if k % 512:
        return np.exp2(np.random.permutation(np.resize(levels, k // 32))).repeat(32)
    a = np.empty((k // 512, 16))
    for p in range(k // 512):
        a[p, :8] = np.random.permutation(np.resize(levels, 8))
        for g in range(8):
            far = levels[np.abs(levels - a[p, g]) >= 10]
            a[p, g + 8] = far[np.random.randint(len(far))]
    return np.exp2(a.ravel()).repeat(32)


BF16 = ml_dtypes.bfloat16


def bf(x):
    return np.asarray(x, np.float32).astype(BF16)


def f64(x):
    return np.asarray(x).astype(np.float64)


E2M1 = np.array([0.0, 0.5, 1.0, 1.5, 2.0, 3.0, 4.0, 6.0, -0.0, -0.5, -1.0, -1.5, -2.0, -3.0, -4.0, -6.0])


def pack_weight(w, fmt):
    k, n = w.shape
    w = f64(bf(w)).reshape(k // 32, 32, n)
    amax = np.abs(w).max(1)
    if fmt == "e4m3":
        byte = np.frexp(amax)[1] - 1 + 127 - 7
    else:
        mant, ex = np.frexp(amax / 6.0)
        byte = np.where(mant > 0.5, ex, ex - 1) + 127
    byte = np.clip(np.where(amax > 0, byte, 1), 1, 254)
    scaled = (w * np.exp2(127.0 - byte)[:, None, :]).reshape(k, n).astype(np.float32)
    by_word = np.ascontiguousarray(scaled.reshape(k // 512, 128, 4, n).transpose(0, 1, 3, 2))
    if fmt == "e4m3":
        words = by_word.astype(ml_dtypes.float8_e4m3fn).view(np.uint8)
    else:
        c = by_word.astype(ml_dtypes.float4_e2m1fn).view(np.uint8) & 0xF
        words = c[..., 0::2] | (c[..., 1::2] << 4)
    return np.ascontiguousarray(words), np.ascontiguousarray(byte.astype(np.uint8).reshape(k // 512, 16, n))


def unpack_weight(words, scales, fmt):
    g, p, n, _ = words.shape
    if fmt == "e4m3":
        vals = np.ascontiguousarray(words).view(ml_dtypes.float8_e4m3fn).astype(np.float64)
    else:
        nib = np.empty((g, p, n, 4), np.uint8)
        nib[..., 0::2] = words & 0xF
        nib[..., 1::2] = words >> 4
        vals = E2M1[nib]
    vals = vals * np.repeat(np.exp2(scales.astype(np.float64) - 127.0), 8, axis=1)[..., None]
    return vals.transpose(0, 1, 3, 2).reshape(g * 512, n)
def pack4(w):
    words, scales = pack_weight(w, "e2m1")
    return words.reshape(words.shape[0], 128, -1), scales


def unpack4(words, scales):
    return unpack_weight(words.reshape(words.shape[0], 128, -1, 2), scales, "e2m1")


R, M, F, C = 2048, 1536, 1024, 512


def setup_inputs():
    s = mx_kscale(M)
    t = mx_kscale(F)
    groups = np.random.standard_normal((M, F)) / np.sqrt(M) / s[:, None] * t
    groups_words, groups_scales = pack4(groups)
    return {"stoich": bf(np.random.standard_normal((M, R)) * s[:, None]),
            "groups_words": groups_words,
            "groups_scales": groups_scales,
            "half": bf(0.3 * np.random.standard_normal(F) * t),
            "energies": bf(0.5 * np.random.standard_normal((F, C)) / np.sqrt(F) / t[:, None]),
            "shift": bf(0.3 * np.random.standard_normal(R)),
            "beta": bf(1 + 0.1 * np.random.standard_normal(C))}


def reference(stoich, groups_words, groups_scales, half, energies, shift, beta):
    nu = mxq(f64(stoich), 0, "e4m3")
    groups = unpack4(groups_words, groups_scales)
    change = (nu.T @ groups) + f64(half)
    gibbs = (mxq(change, 1, "e5m2") @ mxq(f64(energies), 0, "e4m3")) + f64(shift)[:, None]
    return np.exp(-gibbs * f64(beta))

@@ -1,0 +1,301 @@
+from contextlib import ExitStack
+
+import concourse.mybir as mybir
+from concourse.masks import make_identity
+
+R, M, F, C = 2048, 1536, 1024, 512
+FLOPS = 2 * R * M * F + 2 * R * F * C
+
+F32 = mybir.dt.float32
+BF16 = mybir.dt.bfloat16
+I32 = mybir.dt.int32
+U32 = mybir.dt.uint32
+U8 = mybir.dt.uint8
+E4M3 = mybir.dt.float8_e4m3fn_x4
+E5M2 = mybir.dt.float8_e5m2_x4
+E2M1 = mybir.dt.float4_e2m1fn_x4
+ACT = mybir.ActivationFunctionType
+ALU = mybir.AluOpType
+
+P = 128
+PACK = 4
+K_PASS = P * PACK
+N = 512
+M_PASSES = M // K_PASS
+F_PASSES = F // K_PASS
+CHUNKS = R // N
+UNITS = CHUNKS * F_PASSES
+ROW_TILES = N // P
+RUN = 4
+
+HEAD_TILES = 6
+HEAD_SPLIT = 288
+LATE_SPLIT = 384
+AHEAD = 5
+CHANGE_START = 13
+CHANGE_PACE = 3
+SECOND_START = 23
+SECOND_PACE = 5
+
+
+def tile_reaction_gibbs_constants_s9_kernel(
+    tc, stoich, groups_words, groups_scales, half, energies, shift, beta, out
+):
+    nc = tc.nc
+
+    with ExitStack() as ctx:
+        keep = ctx.enter_context(tc.tile_pool(name="keep", bufs=1))
+        work = ctx.enter_context(tc.tile_pool(name="work", bufs=4))
+        psum = ctx.enter_context(tc.psum_pool(name="psum", bufs=8))
+        ctx.enter_context(tc.manual_schedule())
+
+        rows = keep.tile([P, F_PASSES * P], BF16, name="rows")
+        ident = keep.tile([P, P], BF16, name="ident")
+        warm = keep.tile([P, 1], F32, name="warm")
+        scale_raw = keep.tile([P, M_PASSES, F // 4], I32, name="scale_raw")
+        nc.vector.memset(scale_raw[:], 0)
+        nc.vector.memset(warm[:], 0.0)
+        nc.scalar.activation(out=warm[:], in_=warm[:], func=ACT.Exp)
+        nc.gpsimd.memset(rows[:], 0.0)
+        make_identity(nc, ident[:])
+
+        s_raw = {}
+        w_raw = {}
+        e_raw = {}
+
+        def load_stoich(j, g):
+            s_raw[j, g] = keep.tile([P, PACK, N], BF16, name="s_raw_%d_%d" % (j, g))
+            src = stoich[g * K_PASS : (g + 1) * K_PASS, j * N : (j + 1) * N]
+            nc.sync.dma_start(out=s_raw[j, g][:], in_=src.rearrange("(p t) n -> p t n", t=PACK))
+
+        def load_words(g):
+            w_raw[g] = keep.tile([P, F // 2], I32, name="w_raw_%d" % g)
+            nc.sync.dma_start(out=w_raw[g][:], in_=groups_words[g].bitcast(I32))
+
+        def load_scales():
+            src = groups_scales.bitcast(I32).rearrange("g (q r) n -> r q g n", r=4)
+            for r in range(4):
+                nc.sync.dma_start(out=scale_raw[r:P:32, :, :], in_=src[r])
+
+        def load_energies(h):
+            e_raw[h] = keep.tile([P, PACK, C], BF16, name="e_raw_%d" % h)
+            src = energies[h * K_PASS : (h + 1) * K_PASS, :].rearrange("(u t r) c -> r u t c", t=PACK, r=RUN)
+            for r in range(RUN):
+                nc.sync.dma_start(out=e_raw[h][r:P:RUN, :, :], in_=src[r])
+
+        def load_vectors():
+            nc.sync.dma_start(
+                out=rows[0:4, :].rearrange("t (u r) -> t u r", r=RUN),
+                in_=half.rearrange("(u t r) -> t u r", t=PACK, r=RUN),
+            )
+            nc.sync.dma_start(out=rows[4:20, 0:P], in_=shift.rearrange("(n p) -> n p", p=P))
+            nc.sync.dma_start(out=rows[20:24, 0:P], in_=beta.rearrange("(n p) -> n p", p=P))
+
+        for g in range(M_PASSES):
+            load_stoich(0, g)
+            load_words(g)
+            if g == 0:
+                load_scales()
+            if g == 1:
+                load_vectors()
+        for g in range(M_PASSES):
+            load_stoich(1, g)
+        for h in range(F_PASSES):
+            load_energies(h)
+        for j in range(2, CHUNKS):
+            for g in range(M_PASSES):
+                load_stoich(j, g)
+
+        pending = []
+
+        def flush():
+            for codes, scales, grouped, fmt in pending:
+                nc.vector.quantize_mx(out=codes.bitcast(fmt), scales=scales, in_=grouped)
+            pending.clear()
+
+        def interleave(copy, grouped, raw, c0, c1):
+            copy(
+                out=grouped[:, PACK * c0 : PACK * c1].rearrange("p (c i t) -> p c t i", i=4, t=PACK),
+                in_=raw[:, :, c0:c1].rearrange("p t (c i) -> p c t i", i=4),
+            )
+
+        def operand(name):
+            codes = keep.tile([P, N], U32, name=name + "_codes", align_bytes=64)
+            scales = keep.tile([P, N], U8, name=name + "_scales", align_bytes=64)
+            return codes, scales
+
+        def prepare(raw, name, fmt, split):
+            grouped = work.tile([P, PACK * N], BF16, name="grouped", align_bytes=64)
+            interleave(nc.vector.tensor_copy, grouped, raw, 0, split)
+            interleave(nc.scalar.copy, grouped, raw, split, N)
+            flush()
+            codes, scales = operand(name)
+            pending.append((codes[:], scales[:], grouped[:], fmt))
+            return codes, scales
+
+        w_codes = {}
+        w_scales = {}
+
+        def sort_weights(g):
+            w_codes[g] = keep.tile([P, 2 * F], U8, name="w_codes_%d" % g, align_bytes=64)
+            w_scales[g] = keep.tile([P, F], U8, name="w_scales_%d" % g, align_bytes=64)
+            nc.vector.tensor_copy(
+                out=w_codes[g][:].bitcast(I32).rearrange("p (h t u r) -> p h t u r", h=F_PASSES, t=PACK, r=2),
+                in_=w_raw[g][:].rearrange("p (h u t r) -> p h t u r", h=F_PASSES, t=PACK, r=2),
+            )
+            nc.vector.tensor_copy(
+                out=w_scales[g][:].bitcast(I32).rearrange("p (h t u) -> p h t u", h=F_PASSES, t=PACK),
+                in_=scale_raw[:, g, :].rearrange("p (h u t) -> p h t u", h=F_PASSES, t=PACK),
+            )
+
+        s_mx = {}
+        e_mx = {}
+        c_mx = {}
+        inputs = [("s", j, g) for j in range(2) for g in range(M_PASSES)]
+        inputs = inputs + [("e", 0, h) for h in range(F_PASSES)]
+        inputs = inputs + [("s", j, g) for j in range(2, CHUNKS) for g in range(M_PASSES)]
+
+        def prepare_input(n):
+            kind, j, g = inputs[n]
+            split = HEAD_SPLIT if n < HEAD_TILES else LATE_SPLIT
+            if kind == "s":
+                s_mx[j, g] = prepare(s_raw[j, g], "s_%d_%d" % (j, g), E4M3, split)
+            else:
+                e_mx[g] = prepare(e_raw[g], "e_%d" % g, E4M3, split)
+
+        first_banks = {}
+        change_raw = {}
+
+        def first_pass(u, t, g):
+            j, h = divmod(u, F_PASSES)
+            if g == 0:
+                first_banks[u, t] = psum.tile([P, N], F32, name="bank")
+            f = h * PACK + t
+            codes, scales = s_mx[j, g]
+            nc.tensor.matmul_mx(
+                out=first_banks[u, t][:],
+                lhsT=w_codes[g][:, 2 * P * f : 2 * P * (f + 1)].bitcast(E2M1),
+                lhsT_scale=w_scales[g][:, P * f : P * (f + 1)],
+                rhs=codes[:].bitcast(E4M3),
+                rhs_scale=scales[:],
+                start=(g == 0),
+                stop=(g == M_PASSES - 1),
+            )
+
+        def add_half(u, t):
+            h = u % F_PASSES
+            if t == 0:
+                change_raw[u] = keep.tile([P, PACK, N], BF16, name="change_raw_%d" % u)
+            nc.scalar.activation(
+                out=change_raw[u][:, t, :],
+                in_=first_banks[u, t][:],
+                func=ACT.Identity,
+                bias=cols[:, h, t : t + 1],
+            )
+
+        def prepare_change(u):
+            c_mx[u] = prepare(change_raw[u], "c_%d" % u, E5M2, LATE_SPLIT)
+
+        second_banks = {}
+        scaled = {}
+
+        def second_product(j, i):
+            second_banks[j, i] = psum.tile([P, C], F32, name="bank")
+            for h in range(F_PASSES):
+                codes, scales = c_mx[F_PASSES * j + h]
+                nc.tensor.matmul_mx(
+                    out=second_banks[j, i][:],
+                    lhsT=codes[:, P * i : P * (i + 1)].bitcast(E5M2),
+                    lhsT_scale=scales[:, P * i : P * (i + 1)],
+                    rhs=e_mx[h][0][:].bitcast(E4M3),
+                    rhs_scale=e_mx[h][1][:],
+                    start=(h == 0),
+                    stop=(h == F_PASSES - 1),
+                )
+
+        def shift_and_scale(j, i):
+            n = ROW_TILES * j + i
+            scaled[j, i] = work.tile([P, C], F32, name="scaled")
+            nc.vector.scalar_tensor_tensor(
+                out=scaled[j, i][:],
+                in0=second_banks[j, i][:],
+                scalar=cols[:, 0, 4 + n : 5 + n],
+                in1=beta_rows[:],
+                op0=ALU.add,
+                op1=ALU.mult,
+            )
+
+        def finish(j, i):
+            n = ROW_TILES * j + i
+            result = work.tile([P, C], F32, name="result", bufs=6)
+            nc.scalar.activation(out=result[:], in_=scaled[j, i][:], func=ACT.Exp, scale=-1.0)
+            nc.sync.dma_start(out=out[P * n : P * (n + 1), :], in_=result[:])
+
+        cols = keep.tile([P, F_PASSES, 24], BF16, name="cols")
+        beta_rows = keep.tile([P, C], BF16, name="beta_rows")
+        for g in range(M_PASSES):
+            prepare_input(g)
+            sort_weights(g)
+            flush()
+            for t in range(PACK):
+                first_pass(0, t, g)
+            if g == 0:
+                turned = psum.tile([P, F_PASSES * P], BF16, name="bank")
+                for h in range(F_PASSES):
+                    nc.tensor.transpose(turned[:, P * h : P * (h + 1)], rows[:, P * h : P * (h + 1)], ident[:])
+        nc.scalar.copy(out=cols[:], in_=turned[:].rearrange("p (h n) -> p h n", h=F_PASSES)[:, :, 0:24])
+        spread = psum.tile([P, C], BF16, name="bank")
+        for m in range(C // P):
+            nc.tensor.transpose(
+                spread[:, P * m : P * (m + 1)],
+                cols[:, 0, 20 + m : 21 + m].to_broadcast([P, P]),
+                ident[:],
+            )
+        for n in range(M_PASSES, AHEAD):
+            prepare_input(n)
+        nc.scalar.copy(out=beta_rows[:], in_=spread[:])
+
+        steps = UNITS * PACK
+        change_at = {max(PACK * (u + 1), CHANGE_START + CHANGE_PACE * u): u for u in range(UNITS - 1)}
+        second_at = {min(steps - 1, SECOND_START + SECOND_PACE * j): j for j in range(CHUNKS - 1)}
+        for s in range(steps + ROW_TILES + 1):
+            if s < steps:
+                u, t = divmod(s, PACK)
+                if u > 0:
+                    for g in range(M_PASSES):
+                        first_pass(u, t, g)
+                add_half(u, t)
+            if AHEAD + s < len(inputs):
+                prepare_input(AHEAD + s)
+            if s in change_at:
+                prepare_change(change_at[s])
+            for s0, j in second_at.items():
+                if 0 <= s - s0 - 1 < ROW_TILES:
+                    shift_and_scale(j, s - s0 - 1)
+            for s0, j in second_at.items():
+                if 0 <= s - s0 - 2 < ROW_TILES:
+                    finish(j, s - s0 - 2)
+            if s in second_at:
+                for i in range(ROW_TILES):
+                    second_product(second_at[s], i)
+
+        last = UNITS - 1
+        c_mx[last] = operand("c_%d" % last)
+        grouped = work.tile([P, PACK * N], BF16, name="grouped", align_bytes=64)
+        for i in range(ROW_TILES):
+            interleave(nc.vector.tensor_copy, grouped, change_raw[last], P * i, P * (i + 1))
+            flush()
+            pending.append(
+                (
+                    c_mx[last][0][:, P * i : P * (i + 1)],
+                    c_mx[last][1][:, P * i : P * (i + 1)],
+                    grouped[:, PACK * P * i : PACK * P * (i + 1)],
+                    E5M2,
+                )
+            )
+        flush()
+        for i in range(ROW_TILES):
+            second_product(CHUNKS - 1, i)
+        for i in range(ROW_TILES):
+            shift_and_scale(CHUNKS - 1, i)
+            finish(CHUNKS - 1, i)

@@ -27,15 +27,23 @@ CHUNKS = R // N
 UNITS = CHUNKS * F_PASSES
 ROW_TILES = N // P
 RUN = 4
+SLOTS = F_PASSES * PACK
+SHIFT_ROW = 32
+BETA_ROW = SHIFT_ROW + CHUNKS
+LIVE_ROWS = BETA_ROW + 2
 
-HEAD_TILES = 6
-HEAD_SPLIT = 288
-LATE_SPLIT = 384
-AHEAD = 5
-CHANGE_START = 13
-CHANGE_PACE = 3
+ENERGIES_AFTER = 9
+HEAD_TILES = 4
+HEAD_SPLIT = 320
+INPUT_SPLIT = 400
+CHANGE_SPLIT = 352
+INPUT_START = 0
+INPUT_PACE = 2
+CHANGE_START = 15
+CHANGE_PACE = 2
 SECOND_START = 23
-SECOND_PACE = 5
+SECOND_PACE = 6
+TAIL_SCALAR = ()
 
 
 def tile_reaction_gibbs_constants_s9_kernel(
@@ -49,7 +57,8 @@ def tile_reaction_gibbs_constants_s9_kernel(
         psum = ctx.enter_context(tc.psum_pool(name="psum", bufs=8))
         ctx.enter_context(tc.manual_schedule())
 
-        rows = keep.tile([P, F_PASSES * P], BF16, name="rows")
+        rows = keep.tile([P, PACK * P], BF16, name="rows")
+        half_raw = keep.tile([P, K_PASS], BF16, name="half_raw")
         ident = keep.tile([P, P], BF16, name="ident")
         warm = keep.tile([P, 1], F32, name="warm")
         scale_raw = keep.tile([P, M_PASSES, F // 4], I32, name="scale_raw")
@@ -59,14 +68,22 @@ def tile_reaction_gibbs_constants_s9_kernel(
         nc.gpsimd.memset(rows[:], 0.0)
         make_identity(nc, ident[:])
 
-        s_raw = {}
+        inputs = [("s", j, g) for j in range(CHUNKS) for g in range(M_PASSES)]
+        inputs = inputs[:ENERGIES_AFTER] + [("e", 0, h) for h in range(F_PASSES)] + inputs[ENERGIES_AFTER:]
+        raws = []
         w_raw = {}
-        e_raw = {}
 
-        def load_stoich(j, g):
-            s_raw[j, g] = keep.tile([P, PACK, N], BF16, name="s_raw_%d_%d" % (j, g))
-            src = stoich[g * K_PASS : (g + 1) * K_PASS, j * N : (j + 1) * N]
-            nc.sync.dma_start(out=s_raw[j, g][:], in_=src.rearrange("(p t) n -> p t n", t=PACK))
+        def load_input(n):
+            kind, j, g = inputs[n]
+            raw = keep.tile([P, PACK, N], BF16, name="%s_raw_%d_%d" % (kind, j, g))
+            raws.append(raw)
+            if kind == "s":
+                src = stoich[g * K_PASS : (g + 1) * K_PASS, j * N : (j + 1) * N]
+                nc.sync.dma_start(out=raw[:], in_=src.rearrange("(p t) n -> p t n", t=PACK))
+            else:
+                src = energies[g * K_PASS : (g + 1) * K_PASS, :].rearrange("(u t r) c -> r u t c", t=PACK, r=RUN)
+                for r in range(RUN):
+                    nc.sync.dma_start(out=raw[r:P:RUN, :, :], in_=src[r])
 
         def load_words(g):
             w_raw[g] = keep.tile([P, F // 2], I32, name="w_raw_%d" % g)
@@ -77,34 +94,20 @@ def tile_reaction_gibbs_constants_s9_kernel(
             for r in range(4):
                 nc.sync.dma_start(out=scale_raw[r:P:32, :, :], in_=src[r])
 
-        def load_energies(h):
-            e_raw[h] = keep.tile([P, PACK, C], BF16, name="e_raw_%d" % h)
-            src = energies[h * K_PASS : (h + 1) * K_PASS, :].rearrange("(u t r) c -> r u t c", t=PACK, r=RUN)
-            for r in range(RUN):
-                nc.sync.dma_start(out=e_raw[h][r:P:RUN, :, :], in_=src[r])
-
         def load_vectors():
-            nc.sync.dma_start(
-                out=rows[0:4, :].rearrange("t (u r) -> t u r", r=RUN),
-                in_=half.rearrange("(u t r) -> t u r", t=PACK, r=RUN),
-            )
-            nc.sync.dma_start(out=rows[4:20, 0:P], in_=shift.rearrange("(n p) -> n p", p=P))
-            nc.sync.dma_start(out=rows[20:24, 0:P], in_=beta.rearrange("(n p) -> n p", p=P))
+            nc.sync.dma_start(out=half_raw[0:F_PASSES, :], in_=half.rearrange("(h k) -> h k", h=F_PASSES))
+            nc.sync.dma_start(out=rows[SHIFT_ROW : SHIFT_ROW + CHUNKS, :], in_=shift.rearrange("(j n) -> j n", n=N))
+            nc.sync.dma_start(out=rows[BETA_ROW : BETA_ROW + 1, :], in_=beta.rearrange("(j c) -> j c", j=1))
 
-        for g in range(M_PASSES):
-            load_stoich(0, g)
-            load_words(g)
-            if g == 0:
+        for n in range(len(inputs)):
+            load_input(n)
+            if n == 0:
+                load_words(0)
                 load_scales()
-            if g == 1:
+            if n == 1:
                 load_vectors()
-        for g in range(M_PASSES):
-            load_stoich(1, g)
-        for h in range(F_PASSES):
-            load_energies(h)
-        for j in range(2, CHUNKS):
-            for g in range(M_PASSES):
-                load_stoich(j, g)
+            if n + 1 < M_PASSES:
+                load_words(n + 1)
 
         pending = []
 
@@ -113,10 +116,10 @@ def tile_reaction_gibbs_constants_s9_kernel(
                 nc.vector.quantize_mx(out=codes.bitcast(fmt), scales=scales, in_=grouped)
             pending.clear()
 
-        def interleave(copy, grouped, raw, c0, c1):
+        def interleave(copy, grouped, raw):
             copy(
-                out=grouped[:, PACK * c0 : PACK * c1].rearrange("p (c i t) -> p c t i", i=4, t=PACK),
-                in_=raw[:, :, c0:c1].rearrange("p t (c i) -> p c t i", i=4),
+                out=grouped.rearrange("p (c i t) -> p c t i", i=4, t=PACK),
+                in_=raw.rearrange("p t (c i) -> p c t i", i=4),
             )
 
         def operand(name):
@@ -124,44 +127,35 @@ def tile_reaction_gibbs_constants_s9_kernel(
             scales = keep.tile([P, N], U8, name=name + "_scales", align_bytes=64)
             return codes, scales
 
-        def prepare(raw, name, fmt, split):
+        def prepare(raw, split, name, fmt):
             grouped = work.tile([P, PACK * N], BF16, name="grouped", align_bytes=64)
-            interleave(nc.vector.tensor_copy, grouped, raw, 0, split)
-            interleave(nc.scalar.copy, grouped, raw, split, N)
+            interleave(nc.vector.tensor_copy, grouped[:, 0 : PACK * split], raw[:, :, 0:split])
+            interleave(nc.scalar.copy, grouped[:, PACK * split : PACK * N], raw[:, :, split:N])
             flush()
             codes, scales = operand(name)
             pending.append((codes[:], scales[:], grouped[:], fmt))
             return codes, scales
 
         w_codes = {}
-        w_scales = {}
+        w_scales = keep.tile([P, M_PASSES, F], U8, name="w_scales", align_bytes=64)
 
-        def sort_weights(g):
+        def sort_words(g):
             w_codes[g] = keep.tile([P, 2 * F], U8, name="w_codes_%d" % g, align_bytes=64)
-            w_scales[g] = keep.tile([P, F], U8, name="w_scales_%d" % g, align_bytes=64)
             nc.vector.tensor_copy(
                 out=w_codes[g][:].bitcast(I32).rearrange("p (h t u r) -> p h t u r", h=F_PASSES, t=PACK, r=2),
                 in_=w_raw[g][:].rearrange("p (h u t r) -> p h t u r", h=F_PASSES, t=PACK, r=2),
             )
+
+        def sort_scales():
             nc.vector.tensor_copy(
-                out=w_scales[g][:].bitcast(I32).rearrange("p (h t u) -> p h t u", h=F_PASSES, t=PACK),
-                in_=scale_raw[:, g, :].rearrange("p (h u t) -> p h t u", h=F_PASSES, t=PACK),
+                out=w_scales[:].bitcast(I32).rearrange("p g (h t u) -> p (g h) t u", h=F_PASSES, t=PACK),
+                in_=scale_raw[:].rearrange("p g (h u t) -> p (g h) t u", h=F_PASSES, t=PACK),
             )
 
-        s_mx = {}
-        e_mx = {}
-        c_mx = {}
-        inputs = [("s", j, g) for j in range(2) for g in range(M_PASSES)]
-        inputs = inputs + [("e", 0, h) for h in range(F_PASSES)]
-        inputs = inputs + [("s", j, g) for j in range(2, CHUNKS) for g in range(M_PASSES)]
+        mx = {}
 
         def prepare_input(n):
-            kind, j, g = inputs[n]
-            split = HEAD_SPLIT if n < HEAD_TILES else LATE_SPLIT
-            if kind == "s":
-                s_mx[j, g] = prepare(s_raw[j, g], "s_%d_%d" % (j, g), E4M3, split)
-            else:
-                e_mx[g] = prepare(e_raw[g], "e_%d" % g, E4M3, split)
+            mx[inputs[n]] = prepare(raws[n], HEAD_SPLIT if n < HEAD_TILES else INPUT_SPLIT, "%s_%d_%d" % inputs[n], E4M3)
 
         first_banks = {}
         change_raw = {}
@@ -171,11 +165,11 @@ def tile_reaction_gibbs_constants_s9_kernel(
             if g == 0:
                 first_banks[u, t] = psum.tile([P, N], F32, name="bank")
             f = h * PACK + t
-            codes, scales = s_mx[j, g]
+            codes, scales = mx["s", j, g]
             nc.tensor.matmul_mx(
                 out=first_banks[u, t][:],
                 lhsT=w_codes[g][:, 2 * P * f : 2 * P * (f + 1)].bitcast(E2M1),
-                lhsT_scale=w_scales[g][:, P * f : P * (f + 1)],
+                lhsT_scale=w_scales[:, g, P * f : P * (f + 1)],
                 rhs=codes[:].bitcast(E4M3),
                 rhs_scale=scales[:],
                 start=(g == 0),
@@ -190,11 +184,12 @@ def tile_reaction_gibbs_constants_s9_kernel(
                 out=change_raw[u][:, t, :],
                 in_=first_banks[u, t][:],
                 func=ACT.Identity,
-                bias=cols[:, h, t : t + 1],
+                bias=cols[:, t, h : h + 1],
             )
 
         def prepare_change(u):
-            c_mx[u] = prepare(change_raw[u], "c_%d" % u, E5M2, LATE_SPLIT)
+            j, h = divmod(u, F_PASSES)
+            mx["c", j, h] = prepare(change_raw[u], CHANGE_SPLIT, "c_%d" % u, E5M2)
 
         second_banks = {}
         scaled = {}
@@ -202,62 +197,85 @@ def tile_reaction_gibbs_constants_s9_kernel(
         def second_product(j, i):
             second_banks[j, i] = psum.tile([P, C], F32, name="bank")
             for h in range(F_PASSES):
-                codes, scales = c_mx[F_PASSES * j + h]
+                codes, scales = mx["c", j, h]
                 nc.tensor.matmul_mx(
                     out=second_banks[j, i][:],
                     lhsT=codes[:, P * i : P * (i + 1)].bitcast(E5M2),
                     lhsT_scale=scales[:, P * i : P * (i + 1)],
-                    rhs=e_mx[h][0][:].bitcast(E4M3),
-                    rhs_scale=e_mx[h][1][:],
+                    rhs=mx["e", 0, h][0][:].bitcast(E4M3),
+                    rhs_scale=mx["e", 0, h][1][:],
                     start=(h == 0),
                     stop=(h == F_PASSES - 1),
                 )
 
+        def group(j):
+            return 2 if j < CHUNKS - 1 else 1
+
         def shift_and_scale(j, i):
-            n = ROW_TILES * j + i
-            scaled[j, i] = work.tile([P, C], F32, name="scaled")
+            if i % group(j) == 0:
+                scaled[j, i // group(j)] = work.tile([P, 2, C], F32, name="scaled", bufs=3)
             nc.vector.scalar_tensor_tensor(
-                out=scaled[j, i][:],
+                out=scaled[j, i // group(j)][:, i % group(j), :],
                 in0=second_banks[j, i][:],
-                scalar=cols[:, 0, 4 + n : 5 + n],
+                scalar=cols[:, i, SHIFT_ROW + j : SHIFT_ROW + j + 1],
                 in1=beta_rows[:],
                 op0=ALU.add,
                 op1=ALU.mult,
             )
+            flush()
 
         def finish(j, i):
-            n = ROW_TILES * j + i
-            result = work.tile([P, C], F32, name="result", bufs=6)
-            nc.scalar.activation(out=result[:], in_=scaled[j, i][:], func=ACT.Exp, scale=-1.0)
-            nc.sync.dma_start(out=out[P * n : P * (n + 1), :], in_=result[:])
+            size = group(j)
+            if i % size < size - 1:
+                return
+            n = ROW_TILES * j + i + 1 - size
+            result = work.tile([P, 2, C], F32, name="result", bufs=4)
+            nc.scalar.activation(
+                out=result[:, 0:size, :], in_=scaled[j, i // size][:, 0:size, :], func=ACT.Exp, scale=-1.0
+            )
+            nc.sync.dma_start(
+                out=out[P * n : P * (n + size), :].rearrange("(i p) c -> p i c", p=P), in_=result[:, 0:size, :]
+            )
 
-        cols = keep.tile([P, F_PASSES, 24], BF16, name="cols")
+        cols = keep.tile([P, PACK, LIVE_ROWS], BF16, name="cols")
         beta_rows = keep.tile([P, C], BF16, name="beta_rows")
         for g in range(M_PASSES):
+            if g == M_PASSES - 1:
+                nc.scalar.copy(
+                    out=rows[0:F_PASSES, :].rearrange("h (t u r) -> h t u r", t=PACK, r=RUN),
+                    in_=half_raw[0:F_PASSES, :].rearrange("h (u t r) -> h t u r", t=PACK, r=RUN),
+                )
             prepare_input(g)
-            sort_weights(g)
+            if g == 0:
+                sort_words(0)
             flush()
+            if g == 0:
+                sort_scales()
+            if g + 1 < M_PASSES:
+                sort_words(g + 1)
+            if g == M_PASSES - 1:
+                turned = psum.tile([P, PACK, P], BF16, name="bank")
+                for t in range(PACK):
+                    nc.tensor.transpose(turned[:, t, :], rows[:, P * t : P * (t + 1)], ident[:])
             for t in range(PACK):
                 first_pass(0, t, g)
-            if g == 0:
-                turned = psum.tile([P, F_PASSES * P], BF16, name="bank")
-                for h in range(F_PASSES):
-                    nc.tensor.transpose(turned[:, P * h : P * (h + 1)], rows[:, P * h : P * (h + 1)], ident[:])
-        nc.scalar.copy(out=cols[:], in_=turned[:].rearrange("p (h n) -> p h n", h=F_PASSES)[:, :, 0:24])
-        spread = psum.tile([P, C], BF16, name="bank")
-        for m in range(C // P):
-            nc.tensor.transpose(
-                spread[:, P * m : P * (m + 1)],
-                cols[:, 0, 20 + m : 21 + m].to_broadcast([P, P]),
-                ident[:],
-            )
-        for n in range(M_PASSES, AHEAD):
-            prepare_input(n)
-        nc.scalar.copy(out=beta_rows[:], in_=spread[:])
+        prepare_input(M_PASSES)
+        nc.scalar.copy(out=cols[:], in_=turned[:, :, 0:LIVE_ROWS])
+
+        def spread_beta():
+            spread = psum.tile([P, C], BF16, name="bank")
+            for m in range(C // P):
+                nc.tensor.transpose(
+                    spread[:, P * m : P * (m + 1)],
+                    cols[:, m, BETA_ROW : BETA_ROW + 1].to_broadcast([P, P]),
+                    ident[:],
+                )
+            nc.scalar.copy(out=beta_rows[:], in_=spread[:])
 
         steps = UNITS * PACK
+        input_at = {INPUT_START + INPUT_PACE * n: M_PASSES + 1 + n for n in range(len(inputs) - M_PASSES - 1)}
         change_at = {max(PACK * (u + 1), CHANGE_START + CHANGE_PACE * u): u for u in range(UNITS - 1)}
-        second_at = {min(steps - 1, SECOND_START + SECOND_PACE * j): j for j in range(CHUNKS - 1)}
+        second_at = [min(steps - 1, SECOND_START + SECOND_PACE * j) for j in range(CHUNKS - 1)]
         for s in range(steps + ROW_TILES + 1):
             if s < steps:
                 u, t = divmod(s, PACK)
@@ -265,34 +283,31 @@ def tile_reaction_gibbs_constants_s9_kernel(
                     for g in range(M_PASSES):
                         first_pass(u, t, g)
                 add_half(u, t)
-            if AHEAD + s < len(inputs):
-                prepare_input(AHEAD + s)
+            if s == 2 * PACK - 1:
+                spread_beta()
+            if s in input_at:
+                prepare_input(input_at[s])
             if s in change_at:
                 prepare_change(change_at[s])
-            for s0, j in second_at.items():
-                if 0 <= s - s0 - 1 < ROW_TILES:
-                    shift_and_scale(j, s - s0 - 1)
-            for s0, j in second_at.items():
-                if 0 <= s - s0 - 2 < ROW_TILES:
-                    finish(j, s - s0 - 2)
+            for j in range(CHUNKS - 1):
+                if 0 <= s - second_at[j] - 1 < ROW_TILES:
+                    shift_and_scale(j, s - second_at[j] - 1)
+            for j in range(CHUNKS - 1):
+                if 0 <= s - second_at[j] - 2 < ROW_TILES:
+                    finish(j, s - second_at[j] - 2)
             if s in second_at:
                 for i in range(ROW_TILES):
-                    second_product(second_at[s], i)
+                    second_product(second_at.index(s), i)
 
-        last = UNITS - 1
-        c_mx[last] = operand("c_%d" % last)
+        codes, scales = operand("c_last")
+        mx["c", CHUNKS - 1, F_PASSES - 1] = (codes, scales)
         grouped = work.tile([P, PACK * N], BF16, name="grouped", align_bytes=64)
         for i in range(ROW_TILES):
-            interleave(nc.vector.tensor_copy, grouped, change_raw[last], P * i, P * (i + 1))
+            part = grouped[:, PACK * P * i : PACK * P * (i + 1)]
+            copy = nc.scalar.copy if i in TAIL_SCALAR else nc.vector.tensor_copy
+            interleave(copy, part, change_raw[UNITS - 1][:, :, P * i : P * (i + 1)])
             flush()
-            pending.append(
-                (
-                    c_mx[last][0][:, P * i : P * (i + 1)],
-                    c_mx[last][1][:, P * i : P * (i + 1)],
-                    grouped[:, PACK * P * i : PACK * P * (i + 1)],
-                    E5M2,
-                )
-            )
+            pending.append((codes[:, P * i : P * (i + 1)], scales[:, P * i : P * (i + 1)], part, E5M2))
         flush()
         for i in range(ROW_TILES):
             second_product(CHUNKS - 1, i)

@@ -25,25 +25,28 @@ M_PASSES = M // K_PASS
 F_PASSES = F // K_PASS
 CHUNKS = R // N
 UNITS = CHUNKS * F_PASSES
+STEPS = UNITS * PACK
+CHUNK_STEPS = F_PASSES * PACK
 ROW_TILES = N // P
 RUN = 4
-SLOTS = F_PASSES * PACK
-SHIFT_ROW = 32
+WALK = 4
+QUADRANT = 32
+SCALE_ROWS = 4
+
+SHIFT_ROW = QUADRANT
 BETA_ROW = SHIFT_ROW + CHUNKS
 LIVE_ROWS = BETA_ROW + 2
 
-ENERGIES_AFTER = 9
-HEAD_TILES = 4
 HEAD_SPLIT = 320
 INPUT_SPLIT = 400
 CHANGE_SPLIT = 352
-INPUT_START = 0
-INPUT_PACE = 2
-CHANGE_START = 15
-CHANGE_PACE = 2
-SECOND_START = 23
+
+HEAD_TILES = M_PASSES + 1
+ENERGIES_AFTER = (CHUNKS - 1) * M_PASSES
+PACE = 2
+CHANGE_START = 2 * CHUNK_STEPS - 1
+SECOND_START = (CHUNKS - 1) * CHUNK_STEPS - 1
 SECOND_PACE = 6
-TAIL_SCALAR = ()
 
 
 def tile_reaction_gibbs_constants_s9_kernel(
@@ -60,11 +63,8 @@ def tile_reaction_gibbs_constants_s9_kernel(
         rows = keep.tile([P, PACK * P], BF16, name="rows")
         half_raw = keep.tile([P, K_PASS], BF16, name="half_raw")
         ident = keep.tile([P, P], BF16, name="ident")
-        warm = keep.tile([P, 1], F32, name="warm")
         scale_raw = keep.tile([P, M_PASSES, F // 4], I32, name="scale_raw")
         nc.vector.memset(scale_raw[:], 0)
-        nc.vector.memset(warm[:], 0.0)
-        nc.scalar.activation(out=warm[:], in_=warm[:], func=ACT.Exp)
         nc.gpsimd.memset(rows[:], 0.0)
         make_identity(nc, ident[:])
 
@@ -74,14 +74,15 @@ def tile_reaction_gibbs_constants_s9_kernel(
         w_raw = {}
 
         def load_input(n):
-            kind, j, g = inputs[n]
-            raw = keep.tile([P, PACK, N], BF16, name="%s_raw_%d_%d" % (kind, j, g))
+            kind, j, which = inputs[n]
+            raw = keep.tile([P, PACK, N], BF16, name="%s_raw_%d_%d" % inputs[n])
             raws.append(raw)
+            k_rows = slice(which * K_PASS, (which + 1) * K_PASS)
             if kind == "s":
-                src = stoich[g * K_PASS : (g + 1) * K_PASS, j * N : (j + 1) * N]
+                src = stoich[k_rows, j * N : (j + 1) * N]
                 nc.sync.dma_start(out=raw[:], in_=src.rearrange("(p t) n -> p t n", t=PACK))
             else:
-                src = energies[g * K_PASS : (g + 1) * K_PASS, :].rearrange("(u t r) c -> r u t c", t=PACK, r=RUN)
+                src = energies[k_rows, :].rearrange("(a t r) c -> r a t c", t=PACK, r=RUN)
                 for r in range(RUN):
                     nc.sync.dma_start(out=raw[r:P:RUN, :, :], in_=src[r])
 
@@ -90,9 +91,9 @@ def tile_reaction_gibbs_constants_s9_kernel(
             nc.sync.dma_start(out=w_raw[g][:], in_=groups_words[g].bitcast(I32))
 
         def load_scales():
-            src = groups_scales.bitcast(I32).rearrange("g (q r) n -> r q g n", r=4)
-            for r in range(4):
-                nc.sync.dma_start(out=scale_raw[r:P:32, :, :], in_=src[r])
+            src = groups_scales.bitcast(I32).rearrange("g (quad row) n -> row quad g n", row=SCALE_ROWS)
+            for row in range(SCALE_ROWS):
+                nc.sync.dma_start(out=scale_raw[row:P:QUADRANT, :, :], in_=src[row])
 
         def load_vectors():
             nc.sync.dma_start(out=half_raw[0:F_PASSES, :], in_=half.rearrange("(h k) -> h k", h=F_PASSES))
@@ -118,8 +119,8 @@ def tile_reaction_gibbs_constants_s9_kernel(
 
         def interleave(copy, grouped, raw):
             copy(
-                out=grouped.rearrange("p (c i t) -> p c t i", i=4, t=PACK),
-                in_=raw.rearrange("p t (c i) -> p c t i", i=4),
+                out=grouped.rearrange("p (c w t) -> p c t w", w=WALK, t=PACK),
+                in_=raw.rearrange("p t (c w) -> p c t w", w=WALK),
             )
 
         def operand(name):
@@ -142,20 +143,21 @@ def tile_reaction_gibbs_constants_s9_kernel(
         def sort_words(g):
             w_codes[g] = keep.tile([P, 2 * F], U8, name="w_codes_%d" % g, align_bytes=64)
             nc.vector.tensor_copy(
-                out=w_codes[g][:].bitcast(I32).rearrange("p (h t u r) -> p h t u r", h=F_PASSES, t=PACK, r=2),
-                in_=w_raw[g][:].rearrange("p (h u t r) -> p h t u r", h=F_PASSES, t=PACK, r=2),
+                out=w_codes[g][:].bitcast(I32).rearrange("p (h t a x) -> p h t a x", h=F_PASSES, t=PACK, x=RUN // 2),
+                in_=w_raw[g][:].rearrange("p (h a t x) -> p h t a x", h=F_PASSES, t=PACK, x=RUN // 2),
             )
 
         def sort_scales():
             nc.vector.tensor_copy(
-                out=w_scales[:].bitcast(I32).rearrange("p g (h t u) -> p (g h) t u", h=F_PASSES, t=PACK),
-                in_=scale_raw[:].rearrange("p g (h u t) -> p (g h) t u", h=F_PASSES, t=PACK),
+                out=w_scales[:].bitcast(I32).rearrange("p g (h t a) -> p (g h) t a", h=F_PASSES, t=PACK),
+                in_=scale_raw[:].rearrange("p g (h a t) -> p (g h) t a", h=F_PASSES, t=PACK),
             )
 
         mx = {}
 
         def prepare_input(n):
-            mx[inputs[n]] = prepare(raws[n], HEAD_SPLIT if n < HEAD_TILES else INPUT_SPLIT, "%s_%d_%d" % inputs[n], E4M3)
+            split = HEAD_SPLIT if n < HEAD_TILES else INPUT_SPLIT
+            mx[inputs[n]] = prepare(raws[n], split, "%s_%d_%d" % inputs[n], E4M3)
 
         first_banks = {}
         change_raw = {}
@@ -164,12 +166,12 @@ def tile_reaction_gibbs_constants_s9_kernel(
             j, h = divmod(u, F_PASSES)
             if g == 0:
                 first_banks[u, t] = psum.tile([P, N], F32, name="bank")
-            f = h * PACK + t
+            column = P * (h * PACK + t)
             codes, scales = mx["s", j, g]
             nc.tensor.matmul_mx(
                 out=first_banks[u, t][:],
-                lhsT=w_codes[g][:, 2 * P * f : 2 * P * (f + 1)].bitcast(E2M1),
-                lhsT_scale=w_scales[:, g, P * f : P * (f + 1)],
+                lhsT=w_codes[g][:, 2 * column : 2 * (column + P)].bitcast(E2M1),
+                lhsT_scale=w_scales[:, g, column : column + P],
                 rhs=codes[:].bitcast(E4M3),
                 rhs_scale=scales[:],
                 start=(g == 0),
@@ -208,14 +210,15 @@ def tile_reaction_gibbs_constants_s9_kernel(
                     stop=(h == F_PASSES - 1),
                 )
 
-        def group(j):
+        def tiles_per_store(j):
             return 2 if j < CHUNKS - 1 else 1
 
         def shift_and_scale(j, i):
-            if i % group(j) == 0:
-                scaled[j, i // group(j)] = work.tile([P, 2, C], F32, name="scaled", bufs=3)
+            size = tiles_per_store(j)
+            if i % size == 0:
+                scaled[j, i // size] = work.tile([P, 2, C], F32, name="scaled", bufs=3)
             nc.vector.scalar_tensor_tensor(
-                out=scaled[j, i // group(j)][:, i % group(j), :],
+                out=scaled[j, i // size][:, i % size, :],
                 in0=second_banks[j, i][:],
                 scalar=cols[:, i, SHIFT_ROW + j : SHIFT_ROW + j + 1],
                 in1=beta_rows[:],
@@ -225,16 +228,17 @@ def tile_reaction_gibbs_constants_s9_kernel(
             flush()
 
         def finish(j, i):
-            size = group(j)
+            size = tiles_per_store(j)
             if i % size < size - 1:
                 return
-            n = ROW_TILES * j + i + 1 - size
+            first_tile = ROW_TILES * j + i + 1 - size
             result = work.tile([P, 2, C], F32, name="result", bufs=4)
             nc.scalar.activation(
                 out=result[:, 0:size, :], in_=scaled[j, i // size][:, 0:size, :], func=ACT.Exp, scale=-1.0
             )
             nc.sync.dma_start(
-                out=out[P * n : P * (n + size), :].rearrange("(i p) c -> p i c", p=P), in_=result[:, 0:size, :]
+                out=out[P * first_tile : P * (first_tile + size), :].rearrange("(i p) c -> p i c", p=P),
+                in_=result[:, 0:size, :],
             )
 
         cols = keep.tile([P, PACK, LIVE_ROWS], BF16, name="cols")
@@ -242,8 +246,8 @@ def tile_reaction_gibbs_constants_s9_kernel(
         for g in range(M_PASSES):
             if g == M_PASSES - 1:
                 nc.scalar.copy(
-                    out=rows[0:F_PASSES, :].rearrange("h (t u r) -> h t u r", t=PACK, r=RUN),
-                    in_=half_raw[0:F_PASSES, :].rearrange("h (u t r) -> h t u r", t=PACK, r=RUN),
+                    out=rows[0:F_PASSES, :].rearrange("h (t a r) -> h t a r", t=PACK, r=RUN),
+                    in_=half_raw[0:F_PASSES, :].rearrange("h (a t r) -> h t a r", t=PACK, r=RUN),
                 )
             prepare_input(g)
             if g == 0:
@@ -255,8 +259,8 @@ def tile_reaction_gibbs_constants_s9_kernel(
                 sort_words(g + 1)
             if g == M_PASSES - 1:
                 turned = psum.tile([P, PACK, P], BF16, name="bank")
-                for t in range(PACK):
-                    nc.tensor.transpose(turned[:, t, :], rows[:, P * t : P * (t + 1)], ident[:])
+                for d in range(PACK):
+                    nc.tensor.transpose(turned[:, d, :], rows[:, P * d : P * (d + 1)], ident[:])
             for t in range(PACK):
                 first_pass(0, t, g)
         prepare_input(M_PASSES)
@@ -264,26 +268,25 @@ def tile_reaction_gibbs_constants_s9_kernel(
 
         def spread_beta():
             spread = psum.tile([P, C], BF16, name="bank")
-            for m in range(C // P):
+            for d in range(C // P):
                 nc.tensor.transpose(
-                    spread[:, P * m : P * (m + 1)],
-                    cols[:, m, BETA_ROW : BETA_ROW + 1].to_broadcast([P, P]),
+                    spread[:, P * d : P * (d + 1)],
+                    cols[:, d, BETA_ROW : BETA_ROW + 1].to_broadcast([P, P]),
                     ident[:],
                 )
             nc.scalar.copy(out=beta_rows[:], in_=spread[:])
 
-        steps = UNITS * PACK
-        input_at = {INPUT_START + INPUT_PACE * n: M_PASSES + 1 + n for n in range(len(inputs) - M_PASSES - 1)}
-        change_at = {max(PACK * (u + 1), CHANGE_START + CHANGE_PACE * u): u for u in range(UNITS - 1)}
-        second_at = [min(steps - 1, SECOND_START + SECOND_PACE * j) for j in range(CHUNKS - 1)]
-        for s in range(steps + ROW_TILES + 1):
-            if s < steps:
+        input_at = {PACE * n: HEAD_TILES + n for n in range(len(inputs) - HEAD_TILES)}
+        change_at = {max(PACK * (u + 1), CHANGE_START + PACE * u): u for u in range(UNITS - 1)}
+        second_at = [min(STEPS - 1, SECOND_START + SECOND_PACE * j) for j in range(CHUNKS - 1)]
+        for s in range(STEPS + ROW_TILES + 1):
+            if s < STEPS:
                 u, t = divmod(s, PACK)
                 if u > 0:
                     for g in range(M_PASSES):
                         first_pass(u, t, g)
                 add_half(u, t)
-            if s == 2 * PACK - 1:
+            if s == CHUNK_STEPS - 1:
                 spread_beta()
             if s in input_at:
                 prepare_input(input_at[s])
@@ -304,8 +307,7 @@ def tile_reaction_gibbs_constants_s9_kernel(
         grouped = work.tile([P, PACK * N], BF16, name="grouped", align_bytes=64)
         for i in range(ROW_TILES):
             part = grouped[:, PACK * P * i : PACK * P * (i + 1)]
-            copy = nc.scalar.copy if i in TAIL_SCALAR else nc.vector.tensor_copy
-            interleave(copy, part, change_raw[UNITS - 1][:, :, P * i : P * (i + 1)])
+            interleave(nc.vector.tensor_copy, part, change_raw[UNITS - 1][:, :, P * i : P * (i + 1)])
             flush()
             pending.append((codes[:, P * i : P * (i + 1)], scales[:, P * i : P * (i + 1)], part, E5M2))
         flush()

from contextlib import ExitStack

import concourse.mybir as mybir
from concourse.masks import make_identity

R, M, F, C = 2048, 1536, 1024, 512
FLOPS = 2 * R * M * F + 2 * R * F * C

F32 = mybir.dt.float32
BF16 = mybir.dt.bfloat16
I32 = mybir.dt.int32
U32 = mybir.dt.uint32
U8 = mybir.dt.uint8
E4M3 = mybir.dt.float8_e4m3fn_x4
E5M2 = mybir.dt.float8_e5m2_x4
E2M1 = mybir.dt.float4_e2m1fn_x4
ACT = mybir.ActivationFunctionType
ALU = mybir.AluOpType

P = 128
PACK = 4
K_PASS = P * PACK
N = 512
M_PASSES = M // K_PASS
F_PASSES = F // K_PASS
CHUNKS = R // N
UNITS = CHUNKS * F_PASSES
STEPS = UNITS * PACK
CHUNK_STEPS = F_PASSES * PACK
ROW_TILES = N // P
RUN = 4
WALK = 4
QUADRANT = 32
SCALE_ROWS = 4

SHIFT_ROW = QUADRANT
BETA_ROW = SHIFT_ROW + CHUNKS
LIVE_ROWS = BETA_ROW + 2

HEAD_SPLIT = 320
INPUT_SPLIT = 400
CHANGE_SPLIT = 352

HEAD_TILES = M_PASSES + 1
ENERGIES_AFTER = (CHUNKS - 1) * M_PASSES
PACE = 2
CHANGE_START = 2 * CHUNK_STEPS - 1
SECOND_START = (CHUNKS - 1) * CHUNK_STEPS - 1
SECOND_PACE = 6


def tile_reaction_gibbs_constants_s9_kernel(
    tc, stoich, groups_words, groups_scales, half, energies, shift, beta, out
):
    nc = tc.nc

    with ExitStack() as ctx:
        keep = ctx.enter_context(tc.tile_pool(name="keep", bufs=1))
        work = ctx.enter_context(tc.tile_pool(name="work", bufs=4))
        psum = ctx.enter_context(tc.psum_pool(name="psum", bufs=8))
        ctx.enter_context(tc.manual_schedule())

        rows = keep.tile([P, PACK * P], BF16, name="rows")
        half_raw = keep.tile([P, K_PASS], BF16, name="half_raw")
        ident = keep.tile([P, P], BF16, name="ident")
        scale_raw = keep.tile([P, M_PASSES, F // 4], I32, name="scale_raw")
        nc.vector.memset(scale_raw[:], 0)
        nc.gpsimd.memset(rows[:], 0.0)
        make_identity(nc, ident[:])

        inputs = [("s", j, g) for j in range(CHUNKS) for g in range(M_PASSES)]
        inputs = inputs[:ENERGIES_AFTER] + [("e", 0, h) for h in range(F_PASSES)] + inputs[ENERGIES_AFTER:]
        raws = []
        w_raw = {}

        def load_input(n):
            kind, j, which = inputs[n]
            raw = keep.tile([P, PACK, N], BF16, name="%s_raw_%d_%d" % inputs[n])
            raws.append(raw)
            k_rows = slice(which * K_PASS, (which + 1) * K_PASS)
            if kind == "s":
                src = stoich[k_rows, j * N : (j + 1) * N]
                nc.sync.dma_start(out=raw[:], in_=src.rearrange("(p t) n -> p t n", t=PACK))
            else:
                src = energies[k_rows, :].rearrange("(a t r) c -> r a t c", t=PACK, r=RUN)
                for r in range(RUN):
                    nc.sync.dma_start(out=raw[r:P:RUN, :, :], in_=src[r])

        def load_words(g):
            w_raw[g] = keep.tile([P, F // 2], I32, name="w_raw_%d" % g)
            nc.sync.dma_start(out=w_raw[g][:], in_=groups_words[g].bitcast(I32))

        def load_scales():
            src = groups_scales.bitcast(I32).rearrange("g (quad row) n -> row quad g n", row=SCALE_ROWS)
            for row in range(SCALE_ROWS):
                nc.sync.dma_start(out=scale_raw[row:P:QUADRANT, :, :], in_=src[row])

        def load_vectors():
            nc.sync.dma_start(out=half_raw[0:F_PASSES, :], in_=half.rearrange("(h k) -> h k", h=F_PASSES))
            nc.sync.dma_start(out=rows[SHIFT_ROW : SHIFT_ROW + CHUNKS, :], in_=shift.rearrange("(j n) -> j n", n=N))
            nc.sync.dma_start(out=rows[BETA_ROW : BETA_ROW + 1, :], in_=beta.rearrange("(j c) -> j c", j=1))

        for n in range(len(inputs)):
            load_input(n)
            if n == 0:
                load_words(0)
                load_scales()
            if n == 1:
                load_vectors()
            if n + 1 < M_PASSES:
                load_words(n + 1)

        pending = []

        def flush():
            for codes, scales, grouped, fmt in pending:
                nc.vector.quantize_mx(out=codes.bitcast(fmt), scales=scales, in_=grouped)
            pending.clear()

        def interleave(copy, grouped, raw):
            copy(
                out=grouped.rearrange("p (c w t) -> p c t w", w=WALK, t=PACK),
                in_=raw.rearrange("p t (c w) -> p c t w", w=WALK),
            )

        def operand(name):
            codes = keep.tile([P, N], U32, name=name + "_codes", align_bytes=64)
            scales = keep.tile([P, N], U8, name=name + "_scales", align_bytes=64)
            return codes, scales

        def prepare(raw, split, name, fmt):
            grouped = work.tile([P, PACK * N], BF16, name="grouped", align_bytes=64)
            interleave(nc.vector.tensor_copy, grouped[:, 0 : PACK * split], raw[:, :, 0:split])
            interleave(nc.scalar.copy, grouped[:, PACK * split : PACK * N], raw[:, :, split:N])
            flush()
            codes, scales = operand(name)
            pending.append((codes[:], scales[:], grouped[:], fmt))
            return codes, scales

        w_codes = {}
        w_scales = keep.tile([P, M_PASSES, F], U8, name="w_scales", align_bytes=64)

        def sort_words(g):
            w_codes[g] = keep.tile([P, 2 * F], U8, name="w_codes_%d" % g, align_bytes=64)
            nc.vector.tensor_copy(
                out=w_codes[g][:].bitcast(I32).rearrange("p (h t a x) -> p h t a x", h=F_PASSES, t=PACK, x=RUN // 2),
                in_=w_raw[g][:].rearrange("p (h a t x) -> p h t a x", h=F_PASSES, t=PACK, x=RUN // 2),
            )

        def sort_scales():
            nc.vector.tensor_copy(
                out=w_scales[:].bitcast(I32).rearrange("p g (h t a) -> p (g h) t a", h=F_PASSES, t=PACK),
                in_=scale_raw[:].rearrange("p g (h a t) -> p (g h) t a", h=F_PASSES, t=PACK),
            )

        mx = {}

        def prepare_input(n):
            split = HEAD_SPLIT if n < HEAD_TILES else INPUT_SPLIT
            mx[inputs[n]] = prepare(raws[n], split, "%s_%d_%d" % inputs[n], E4M3)

        first_banks = {}
        change_raw = {}

        def first_pass(u, t, g):
            j, h = divmod(u, F_PASSES)
            if g == 0:
                first_banks[u, t] = psum.tile([P, N], F32, name="bank")
            column = P * (h * PACK + t)
            codes, scales = mx["s", j, g]
            nc.tensor.matmul_mx(
                out=first_banks[u, t][:],
                lhsT=w_codes[g][:, 2 * column : 2 * (column + P)].bitcast(E2M1),
                lhsT_scale=w_scales[:, g, column : column + P],
                rhs=codes[:].bitcast(E4M3),
                rhs_scale=scales[:],
                start=(g == 0),
                stop=(g == M_PASSES - 1),
            )

        def add_half(u, t):
            h = u % F_PASSES
            if t == 0:
                change_raw[u] = keep.tile([P, PACK, N], BF16, name="change_raw_%d" % u)
            nc.scalar.activation(
                out=change_raw[u][:, t, :],
                in_=first_banks[u, t][:],
                func=ACT.Identity,
                bias=cols[:, t, h : h + 1],
            )

        def prepare_change(u):
            j, h = divmod(u, F_PASSES)
            mx["c", j, h] = prepare(change_raw[u], CHANGE_SPLIT, "c_%d" % u, E5M2)

        second_banks = {}
        scaled = {}

        def second_product(j, i):
            second_banks[j, i] = psum.tile([P, C], F32, name="bank")
            for h in range(F_PASSES):
                codes, scales = mx["c", j, h]
                nc.tensor.matmul_mx(
                    out=second_banks[j, i][:],
                    lhsT=codes[:, P * i : P * (i + 1)].bitcast(E5M2),
                    lhsT_scale=scales[:, P * i : P * (i + 1)],
                    rhs=mx["e", 0, h][0][:].bitcast(E4M3),
                    rhs_scale=mx["e", 0, h][1][:],
                    start=(h == 0),
                    stop=(h == F_PASSES - 1),
                )

        def tiles_per_store(j):
            return 2 if j < CHUNKS - 1 else 1

        def shift_and_scale(j, i):
            size = tiles_per_store(j)
            if i % size == 0:
                scaled[j, i // size] = work.tile([P, 2, C], F32, name="scaled", bufs=3)
            nc.vector.scalar_tensor_tensor(
                out=scaled[j, i // size][:, i % size, :],
                in0=second_banks[j, i][:],
                scalar=cols[:, i, SHIFT_ROW + j : SHIFT_ROW + j + 1],
                in1=beta_rows[:],
                op0=ALU.add,
                op1=ALU.mult,
            )
            flush()

        def finish(j, i):
            size = tiles_per_store(j)
            if i % size < size - 1:
                return
            first_tile = ROW_TILES * j + i + 1 - size
            result = work.tile([P, 2, C], F32, name="result", bufs=4)
            nc.scalar.activation(
                out=result[:, 0:size, :], in_=scaled[j, i // size][:, 0:size, :], func=ACT.Exp, scale=-1.0
            )
            nc.sync.dma_start(
                out=out[P * first_tile : P * (first_tile + size), :].rearrange("(i p) c -> p i c", p=P),
                in_=result[:, 0:size, :],
            )

        cols = keep.tile([P, PACK, LIVE_ROWS], BF16, name="cols")
        beta_rows = keep.tile([P, C], BF16, name="beta_rows")
        for g in range(M_PASSES):
            if g == M_PASSES - 1:
                nc.scalar.copy(
                    out=rows[0:F_PASSES, :].rearrange("h (t a r) -> h t a r", t=PACK, r=RUN),
                    in_=half_raw[0:F_PASSES, :].rearrange("h (a t r) -> h t a r", t=PACK, r=RUN),
                )
            prepare_input(g)
            if g == 0:
                sort_words(0)
            flush()
            if g == 0:
                sort_scales()
            if g + 1 < M_PASSES:
                sort_words(g + 1)
            if g == M_PASSES - 1:
                turned = psum.tile([P, PACK, P], BF16, name="bank")
                for d in range(PACK):
                    nc.tensor.transpose(turned[:, d, :], rows[:, P * d : P * (d + 1)], ident[:])
            for t in range(PACK):
                first_pass(0, t, g)
        prepare_input(M_PASSES)
        nc.scalar.copy(out=cols[:], in_=turned[:, :, 0:LIVE_ROWS])

        def spread_beta():
            spread = psum.tile([P, C], BF16, name="bank")
            for d in range(C // P):
                nc.tensor.transpose(
                    spread[:, P * d : P * (d + 1)],
                    cols[:, d, BETA_ROW : BETA_ROW + 1].to_broadcast([P, P]),
                    ident[:],
                )
            nc.scalar.copy(out=beta_rows[:], in_=spread[:])

        input_at = {PACE * n: HEAD_TILES + n for n in range(len(inputs) - HEAD_TILES)}
        change_at = {max(PACK * (u + 1), CHANGE_START + PACE * u): u for u in range(UNITS - 1)}
        second_at = [min(STEPS - 1, SECOND_START + SECOND_PACE * j) for j in range(CHUNKS - 1)]
        for s in range(STEPS + ROW_TILES + 1):
            if s < STEPS:
                u, t = divmod(s, PACK)
                if u > 0:
                    for g in range(M_PASSES):
                        first_pass(u, t, g)
                add_half(u, t)
            if s == CHUNK_STEPS - 1:
                spread_beta()
            if s in input_at:
                prepare_input(input_at[s])
            if s in change_at:
                prepare_change(change_at[s])
            for j in range(CHUNKS - 1):
                if 0 <= s - second_at[j] - 1 < ROW_TILES:
                    shift_and_scale(j, s - second_at[j] - 1)
            for j in range(CHUNKS - 1):
                if 0 <= s - second_at[j] - 2 < ROW_TILES:
                    finish(j, s - second_at[j] - 2)
            if s in second_at:
                for i in range(ROW_TILES):
                    second_product(second_at.index(s), i)

        codes, scales = operand("c_last")
        mx["c", CHUNKS - 1, F_PASSES - 1] = (codes, scales)
        grouped = work.tile([P, PACK * N], BF16, name="grouped", align_bytes=64)
        for i in range(ROW_TILES):
            part = grouped[:, PACK * P * i : PACK * P * (i + 1)]
            interleave(nc.vector.tensor_copy, part, change_raw[UNITS - 1][:, :, P * i : P * (i + 1)])
            flush()
            pending.append((codes[:, P * i : P * (i + 1)], scales[:, P * i : P * (i + 1)], part, E5M2))
        flush()
        for i in range(ROW_TILES):
            second_product(CHUNKS - 1, i)
        for i in range(ROW_TILES):
            shift_and_scale(CHUNKS - 1, i)
            finish(CHUNKS - 1, i)
